import numpy as np
import ml_dtypes


def mxq(x, axis, fmt="e4m3"):
    dtype, down = {"e4m3": (ml_dtypes.float8_e4m3fn, 7), "e5m2": (ml_dtypes.float8_e5m2, 14)}[fmt]
    v = np.moveaxis(np.asarray(x, np.float32).astype(ml_dtypes.bfloat16).astype(np.float64), axis, -1)
    blocks = v.reshape(v.shape[:-1] + (-1, 32))
    amax = np.abs(blocks).max(-1, keepdims=True)
    byte = np.maximum(np.where(amax > 0, np.frexp(amax)[1] - 1 + 127, 0) - down, 1)
    scale = np.exp2(byte - 127.0)
    codes = (blocks / scale).astype(np.float32).astype(dtype).astype(np.float64)
    return np.moveaxis((codes * scale).reshape(v.shape), -1, axis)


WIDE = False


def mx_kscale(k):
    if not WIDE:
        return np.ones(k)
    levels = np.array([10, -10, 5, -5, 0])
    if k % 512:
        return np.exp2(np.random.permutation(np.resize(levels, k // 32))).repeat(32)
    a = np.empty((k // 512, 16))
    for p in range(k // 512):
        a[p, :8] = np.random.permutation(np.resize(levels, 8))
        for g in range(8):
            far = levels[np.abs(levels - a[p, g]) >= 10]
            a[p, g + 8] = far[np.random.randint(len(far))]
    return np.exp2(a.ravel()).repeat(32)


def f64(x):
    return np.asarray(x).astype(np.float64)


def striped(idx):
    return np.tile(idx.reshape(-1, 16).T, (8, 1)).astype(np.uint16)


def unstriped(offs):
    return offs[:16].T.reshape(-1).astype(np.int64)


def pack_weight(w):
    k, n = w.shape
    w = f64(np.asarray(w, np.float32).astype(ml_dtypes.bfloat16)).reshape(k // 32, 32, n)
    amax = np.abs(w).max(1)
    byte = np.clip(np.where(amax > 0, np.frexp(amax)[1] - 1 + 127 - 7, 1), 1, 254)
    scaled = (w * np.exp2(127.0 - byte)[:, None, :]).reshape(k, n).astype(np.float32)
    words = np.ascontiguousarray(scaled.reshape(k // 512, 128, 4, n).transpose(0, 1, 3, 2)).astype(ml_dtypes.float8_e4m3fn).view(np.uint8)
    return words, np.ascontiguousarray(byte.astype(np.uint8).reshape(k // 512, 16, n))


def unpack_weight(words, scales):
    g, p, n, _ = words.shape
    vals = np.ascontiguousarray(words).view(ml_dtypes.float8_e4m3fn).astype(np.float64) * np.repeat(np.exp2(scales.astype(np.float64) - 127.0), 8, axis=1)[..., None]
    return vals.transpose(0, 1, 3, 2).reshape(g * 512, n)


K, T, S, N = 512, 2048, 1024, 128
P = 2 ** 7


def setup_inputs():
    n = np.random.standard_normal
    s = mx_kscale(K)[:, None]
    packed_xT = pack_weight(n((K, T)) * s)
    return {
        "x_words": packed_xT[0],
        "x_scales": packed_xT[1],
        "w1": (n((K, N)) / np.sqrt(K) / s).astype(np.float32),
        "prior": np.tile(0.5 * np.random.standard_normal(S), (P, 1)).astype(np.float32),
        "offs": striped(np.random.permutation(T)[:S]),
    }


def reference(x_words, x_scales, w1, prior, offs):
    xq = unpack_weight(x_words, x_scales)[:, unstriped(offs)]
    y = mxq(f64(w1), 0, "e4m3").T @ xq
    yp = y + f64(prior)[:1]
    e = np.exp(yp - yp.max(axis=1, keepdims=True))
    return e / e.sum(axis=1, keepdims=True)

@@ -1,0 +1,98 @@
+from contextlib import ExitStack
+
+import concourse.mybir as mybir
+
+K, T, S, M = 512, 2048, 1024, 128
+FLOPS = 2 * K * M * S
+
+F32 = mybir.dt.float32
+BF16 = mybir.dt.bfloat16
+I32 = mybir.dt.int32
+U32 = mybir.dt.uint32
+U16 = mybir.dt.uint16
+U8 = mybir.dt.uint8
+FP8X4 = mybir.dt.float8_e4m3fn_x4
+ALU = mybir.AluOpType
+ACT = mybir.ActivationFunctionType
+AX = mybir.AxisListType
+
+P = 128
+FIRST = 640
+PAD = 4
+BIG = 2.0 ** 126
+
+
+def tile_picked_rank_prior_p_kernel(tc, x_words, x_scales, w1, prior, offs, out):
+    nc = tc.nc
+    with ExitStack() as ctx:
+        keep = ctx.enter_context(tc.tile_pool(name="keep", bufs=1))
+        psum = ctx.enter_context(tc.psum_pool(name="psum", bufs=1))
+
+        offsets = keep.tile([P, S // 16], U16, name="offsets")
+        scale_table = keep.tile([P, T], U8, name="scale_table", align_bytes=64)
+        word_table = keep.tile([P, T], U32, name="word_table", align_bytes=64)
+        w_raw = keep.tile([P, 4, M], F32, name="w_raw")
+        pieces = [(0, 512), (512, 256), (768, 256)]
+        prior_sb = [keep.tile([P, 512], F32, name="prior%d" % h) for h in range(2)]
+
+        nc.vector.memset(scale_table[:].bitcast(I32), 0)
+        nc.sync.dma_start(out=w_raw[:], in_=w1.rearrange("(p j) m -> p j m", j=4))
+        nc.sync.dma_start(offsets[:], offs)
+        for q in range(4):
+            queue = nc.sync if q % 2 == 0 else nc.scalar
+            queue.dma_start(out=scale_table[32 * q : 32 * q + 4, :].bitcast(I32), in_=x_scales[0, 4 * q : 4 * q + 4, :].bitcast(I32))
+        nc.sync.dma_start(out=word_table[:].bitcast(I32), in_=x_words[0].rearrange("p n t -> p (n t)").bitcast(I32))
+        for h in range(2):
+            nc.sync.dma_start(out=prior_sb[h][:], in_=prior[:, h * 512 : (h + 1) * 512])
+
+        w_bf = keep.tile([P, M, 4], BF16, name="w_bf", align_bytes=64)
+        w_codes = keep.tile([P, M], U32, name="w_codes", align_bytes=64)
+        w_scales = keep.tile([P, M], U8, name="w_scales", align_bytes=64)
+        halves = [slice(0, M // 2), slice(M // 2, M)]
+        for m in halves:
+            nc.vector.tensor_copy(out=w_bf[:, m, :].rearrange("p (c i) j -> p c j i", i=4), in_=w_raw[:, :, m].rearrange("p j (c i) -> p c j i", i=4))
+        for m in halves:
+            nc.vector.quantize_mx(out=w_codes[:, m].bitcast(FP8X4), scales=w_scales[:, m], in_=w_bf[:, m, :].rearrange("p m j -> p (m j)"))
+
+        neg = keep.tile([P, PAD + S + 1], F32, name="neg")
+        nc.vector.memset(neg[:, PAD - 1 : PAD], BIG)
+
+        x_bytes = keep.tile([P, S], U8, name="x_bytes", align_bytes=64)
+        nc.vector.tensor_copy(x_bytes[:], scale_table[:].indirect(offsets[:]))
+
+        banks = []
+        for c, (lo, n) in enumerate(pieces):
+            codes = keep.tile([P, n], U32, name="codes%d" % c, align_bytes=64)
+            nc.vector.tensor_copy(codes[:], word_table[:].indirect(offsets[:, lo // 16 : (lo + n) // 16]))
+            bank = psum.tile([P, n], F32, name="bank%d" % c)
+            nc.tensor.matmul_mx(out=bank[:], lhsT=w_codes[:].bitcast(FP8X4), lhsT_scale=w_scales[:], rhs=codes[:].bitcast(FP8X4), rhs_scale=x_bytes[:, lo : lo + n], start=True, stop=True)
+            banks.append(bank)
+
+        for c, (lo, n) in enumerate(pieces):
+            h, o = divmod(lo, 512)
+            nc.vector.scalar_tensor_tensor(out=neg[:, PAD + lo : PAD + lo + n], in0=banks[c][:], scalar=-1.0, in1=prior_sb[h][:, o : o + n], op0=ALU.mult, op1=ALU.subtract)
+
+        stats = keep.tile([P, 8], F32, name="stats")
+        sums = keep.tile([P, 8], F32, name="sums")
+        e = keep.tile([P, S + 1], F32, name="e")
+        neg_max0 = neg[:, PAD + S : PAD + S + 1]
+        nc.vector.tensor_reduce(out=neg_max0, in_=neg[:, PAD - 1 : PAD + FIRST], axis=AX.X, op=ALU.min)
+        nc.scalar.activation(out=e[:, 0:FIRST], in_=neg[:, PAD : PAD + FIRST], func=ACT.Exp, bias=neg_max0, scale=-1.0, accum_out=sums[:, 0:1])
+        nc.vector.tensor_reduce(out=stats[:, 0:1], in_=neg[:, PAD + FIRST : PAD + S + 1], axis=AX.X, op=ALU.min)
+        nc.scalar.activation(out=e[:, FIRST : S + 1], in_=neg[:, PAD + FIRST : PAD + S + 1], func=ACT.Exp, bias=stats[:, 0:1], scale=-1.0, accum_out=sums[:, 1:2])
+        f = e[:, S : S + 1]
+        nc.vector.tensor_scalar(out=stats[:, 1:2], in0=sums[:, 0:1], scalar1=-1.0, scalar2=None, op0=ALU.add)
+        nc.vector.tensor_scalar(out=stats[:, 2:3], in0=f, scalar1=stats[:, 1:2], scalar2=sums[:, 1:2], op0=ALU.mult, op1=ALU.add)
+        nc.vector.reciprocal(out=stats[:, 3:4], in_=stats[:, 2:3])
+        r = stats[:, 3:4]
+        for i, (lo, hi) in enumerate([(0, 256), (256, 640)]):
+            o = keep.tile([P, hi - lo], F32, name="out_v%d" % i)
+            if hi <= FIRST:
+                nc.vector.tensor_scalar(out=o[:], in0=e[:, lo:hi], scalar1=f, scalar2=r, op0=ALU.mult, op1=ALU.mult)
+            else:
+                nc.vector.tensor_scalar(out=o[:], in0=e[:, lo:hi], scalar1=r, scalar2=None, op0=ALU.mult)
+            nc.sync.dma_start(out=out[:, lo:hi], in_=o[:])
+        lo = 640
+        o = keep.tile([P, S - lo], F32, name="out_s")
+        nc.scalar.activation(out=o[:], in_=e[:, lo:S], func=ACT.Copy, scale=r)
+        nc.scalar.dma_start(out=out[:, lo:S], in_=o[:])

@@ -40,7 +40,7 @@ def tile_picked_rank_prior_p_kernel(tc, x_words, x_scales, w1, prior, offs, out)
         nc.sync.dma_start(offsets[:], offs)
         for q in range(4):
             queue = nc.sync if q % 2 == 0 else nc.scalar
-            queue.dma_start(out=scale_table[32 * q : 32 * q + 4, :].bitcast(I32), in_=x_scales[0, 4 * q : 4 * q + 4, :].bitcast(I32))
+            queue.dma_start(out=scale_table[q:P:32, :].bitcast(I32), in_=x_scales[0, q:16:4, :].bitcast(I32))
         nc.sync.dma_start(out=word_table[:].bitcast(I32), in_=x_words[0].rearrange("p n t -> p (n t)").bitcast(I32))
         for h in range(2):
             nc.sync.dma_start(out=prior_sb[h][:], in_=prior[:, h * 512 : (h + 1) * 512])
@@ -85,14 +85,10 @@ def tile_picked_rank_prior_p_kernel(tc, x_words, x_scales, w1, prior, offs, out)
         nc.vector.tensor_scalar(out=stats[:, 2:3], in0=f, scalar1=stats[:, 1:2], scalar2=sums[:, 1:2], op0=ALU.mult, op1=ALU.add)
         nc.vector.reciprocal(out=stats[:, 3:4], in_=stats[:, 2:3])
         r = stats[:, 3:4]
-        for i, (lo, hi) in enumerate([(0, 256), (256, 640)]):
-            o = keep.tile([P, hi - lo], F32, name="out_v%d" % i)
-            if hi <= FIRST:
-                nc.vector.tensor_scalar(out=o[:], in0=e[:, lo:hi], scalar1=f, scalar2=r, op0=ALU.mult, op1=ALU.mult)
-            else:
-                nc.vector.tensor_scalar(out=o[:], in0=e[:, lo:hi], scalar1=r, scalar2=None, op0=ALU.mult)
-            nc.sync.dma_start(out=out[:, lo:hi], in_=o[:])
-        lo = 640
-        o = keep.tile([P, S - lo], F32, name="out_s")
-        nc.scalar.activation(out=o[:], in_=e[:, lo:S], func=ACT.Copy, scale=r)
-        nc.scalar.dma_start(out=out[:, lo:S], in_=o[:])
+        o = keep.tile([P, S], F32, name="o")
+        for lo, hi in ((0, 256), (256, 512), (512, FIRST)):
+            nc.vector.tensor_scalar(out=o[:, lo:hi], in0=e[:, lo:hi], scalar1=f, scalar2=r, op0=ALU.mult, op1=ALU.mult)
+        nc.scalar.activation(out=o[:, FIRST:S], in_=e[:, FIRST:S], func=ACT.Copy, scale=r)
+        nc.sync.dma_start(out=out[:, 0:256], in_=o[:, 0:256])
+        nc.sync.dma_start(out=out[:, 256:512], in_=o[:, 256:512])
+        nc.scalar.dma_start(out=out[:, 512:S], in_=o[:, 512:S])

@@ -39,8 +39,7 @@ def tile_picked_rank_prior_p_kernel(tc, x_words, x_scales, w1, prior, offs, out)
         nc.sync.dma_start(out=w_raw[:], in_=w1.rearrange("(p j) m -> p j m", j=4))
         nc.sync.dma_start(offsets[:], offs)
         for q in range(4):
-            queue = nc.sync if q % 2 == 0 else nc.scalar
-            queue.dma_start(out=scale_table[q:P:32, :].bitcast(I32), in_=x_scales[0, q:16:4, :].bitcast(I32))
+            nc.sync.dma_start(out=scale_table[q:P:32, :].bitcast(I32), in_=x_scales[0, q:16:4, :].bitcast(I32))
         nc.sync.dma_start(out=word_table[:].bitcast(I32), in_=x_words[0].rearrange("p n t -> p (n t)").bitcast(I32))
         for h in range(2):
             nc.sync.dma_start(out=prior_sb[h][:], in_=prior[:, h * 512 : (h + 1) * 512])
@@ -85,10 +84,14 @@ def tile_picked_rank_prior_p_kernel(tc, x_words, x_scales, w1, prior, offs, out)
         nc.vector.tensor_scalar(out=stats[:, 2:3], in0=f, scalar1=stats[:, 1:2], scalar2=sums[:, 1:2], op0=ALU.mult, op1=ALU.add)
         nc.vector.reciprocal(out=stats[:, 3:4], in_=stats[:, 2:3])
         r = stats[:, 3:4]
-        o = keep.tile([P, S], F32, name="o")
-        for lo, hi in ((0, 256), (256, 512), (512, FIRST)):
-            nc.vector.tensor_scalar(out=o[:, lo:hi], in0=e[:, lo:hi], scalar1=f, scalar2=r, op0=ALU.mult, op1=ALU.mult)
-        nc.scalar.activation(out=o[:, FIRST:S], in_=e[:, FIRST:S], func=ACT.Copy, scale=r)
-        nc.sync.dma_start(out=out[:, 0:256], in_=o[:, 0:256])
-        nc.sync.dma_start(out=out[:, 256:512], in_=o[:, 256:512])
-        nc.scalar.dma_start(out=out[:, 512:S], in_=o[:, 512:S])
+        for i, (lo, hi) in enumerate([(0, 256), (256, 640)]):
+            o = keep.tile([P, hi - lo], F32, name="out_v%d" % i)
+            if hi <= FIRST:
+                nc.vector.tensor_scalar(out=o[:], in0=e[:, lo:hi], scalar1=f, scalar2=r, op0=ALU.mult, op1=ALU.mult)
+            else:
+                nc.vector.tensor_scalar(out=o[:], in0=e[:, lo:hi], scalar1=r, scalar2=None, op0=ALU.mult)
+            nc.sync.dma_start(out=out[:, lo:hi], in_=o[:])
+        lo = 640
+        o = keep.tile([P, S - lo], F32, name="out_s")
+        nc.scalar.activation(out=o[:], in_=e[:, lo:S], func=ACT.Copy, scale=r)
+        nc.scalar.dma_start(out=out[:, lo:S], in_=o[:])

@@ -17,9 +17,8 @@ ACT = mybir.ActivationFunctionType
 AX = mybir.AxisListType
 
 P = 128
-FIRST = 640
-PAD = 4
-BIG = 2.0 ** 126
+G = 256
+X = 8
 
 
 def tile_picked_rank_prior_p_kernel(tc, x_words, x_scales, w1, prior, offs, out):
@@ -32,8 +31,7 @@ def tile_picked_rank_prior_p_kernel(tc, x_words, x_scales, w1, prior, offs, out)
         scale_table = keep.tile([P, T], U8, name="scale_table", align_bytes=64)
         word_table = keep.tile([P, T], U32, name="word_table", align_bytes=64)
         w_raw = keep.tile([P, 4, M], F32, name="w_raw")
-        pieces = [(0, 512), (512, 256), (768, 256)]
-        prior_sb = [keep.tile([P, 512], F32, name="prior%d" % h) for h in range(2)]
+        prior_sb = keep.tile([P, S], F32, name="prior_sb")
 
         nc.vector.memset(scale_table[:].bitcast(I32), 0)
         nc.sync.dma_start(out=w_raw[:], in_=w1.rearrange("(p j) m -> p j m", j=4))
@@ -41,8 +39,7 @@ def tile_picked_rank_prior_p_kernel(tc, x_words, x_scales, w1, prior, offs, out)
         for q in range(4):
             nc.sync.dma_start(out=scale_table[q:P:32, :].bitcast(I32), in_=x_scales[0, q:16:4, :].bitcast(I32))
         nc.sync.dma_start(out=word_table[:].bitcast(I32), in_=x_words[0].rearrange("p n t -> p (n t)").bitcast(I32))
-        for h in range(2):
-            nc.sync.dma_start(out=prior_sb[h][:], in_=prior[:, h * 512 : (h + 1) * 512])
+        nc.sync.dma_start(out=prior_sb[:], in_=prior)
 
         w_bf = keep.tile([P, M, 4], BF16, name="w_bf", align_bytes=64)
         w_codes = keep.tile([P, M], U32, name="w_codes", align_bytes=64)
@@ -53,45 +50,52 @@ def tile_picked_rank_prior_p_kernel(tc, x_words, x_scales, w1, prior, offs, out)
         for m in halves:
             nc.vector.quantize_mx(out=w_codes[:, m].bitcast(FP8X4), scales=w_scales[:, m], in_=w_bf[:, m, :].rearrange("p m j -> p (m j)"))
 
-        neg = keep.tile([P, PAD + S + 1], F32, name="neg")
-        nc.vector.memset(neg[:, PAD - 1 : PAD], BIG)
-
         x_bytes = keep.tile([P, S], U8, name="x_bytes", align_bytes=64)
         nc.vector.tensor_copy(x_bytes[:], scale_table[:].indirect(offsets[:]))
 
         banks = []
-        for c, (lo, n) in enumerate(pieces):
+        for c, (lo, n) in enumerate([(g * G, G) for g in range(4)]):
             codes = keep.tile([P, n], U32, name="codes%d" % c, align_bytes=64)
             nc.vector.tensor_copy(codes[:], word_table[:].indirect(offsets[:, lo // 16 : (lo + n) // 16]))
             bank = psum.tile([P, n], F32, name="bank%d" % c)
             nc.tensor.matmul_mx(out=bank[:], lhsT=w_codes[:].bitcast(FP8X4), lhsT_scale=w_scales[:], rhs=codes[:].bitcast(FP8X4), rhs_scale=x_bytes[:, lo : lo + n], start=True, stop=True)
             banks.append(bank)
 
-        for c, (lo, n) in enumerate(pieces):
-            h, o = divmod(lo, 512)
-            nc.vector.scalar_tensor_tensor(out=neg[:, PAD + lo : PAD + lo + n], in0=banks[c][:], scalar=-1.0, in1=prior_sb[h][:, o : o + n], op0=ALU.mult, op1=ALU.subtract)
+        neg_y = [keep.tile([P, X + G], F32, name="neg_y%d" % g, tag="scores%d" % g) for g in range(2)]
+        neg = [keep.tile([P, G], F32, name="neg%d" % g) for g in range(3)]
+        for g in range(2):
+            nc.scalar.activation(out=neg_y[g][:, X:], in_=banks[g][:], func=ACT.Copy, scale=-1.0)
+            nc.gpsimd.tensor_tensor(out=neg[g][:], in0=neg_y[g][:, X:], in1=prior_sb[:, g * G : (g + 1) * G], op=ALU.subtract)
+        neg_last = keep.tile([P, X + G], F32, name="neg_last", tag="scores0")
+        e = [keep.tile([P, G], F32, name="e%d" % g) for g in range(3)]
+        e_last = keep.tile([P, X + G], F32, name="e_last")
+        sums = keep.tile([P, 8], F32, name="sums")
+
+        def add_prior(g, dst):
+            nc.vector.scalar_tensor_tensor(out=dst, in0=banks[g][:], scalar=-1.0, in1=prior_sb[:, g * G : (g + 1) * G], op0=ALU.mult, op1=ALU.subtract)
+
+        def own_softmax(g):
+            col = X - 3 + g
+            nc.vector.tensor_reduce(out=neg_last[:, col : col + 1], in_=neg[g][:], axis=AX.X, op=ALU.min)
+            nc.scalar.activation(out=e[g][:], in_=neg[g][:], func=ACT.Exp, bias=neg_last[:, col : col + 1], scale=-1.0, accum_out=sums[:, 1 + g : 2 + g])
+
+        add_prior(2, neg[2][:])
+        own_softmax(0)
+        own_softmax(2)
+        add_prior(3, neg_last[:, X:])
+        own_softmax(1)
+        nc.vector.tensor_reduce(out=neg_last[:, X - 4 : X - 3], in_=neg_last[:, X - 3 :], axis=AX.X, op=ALU.min)
+        nc.scalar.activation(out=e_last[:, X - 4 :], in_=neg_last[:, X - 4 :], func=ACT.Exp, bias=neg_last[:, X - 4 : X - 3], scale=-1.0, accum_out=sums[:, 0:1])
 
         stats = keep.tile([P, 8], F32, name="stats")
-        sums = keep.tile([P, 8], F32, name="sums")
-        e = keep.tile([P, S + 1], F32, name="e")
-        neg_max0 = neg[:, PAD + S : PAD + S + 1]
-        nc.vector.tensor_reduce(out=neg_max0, in_=neg[:, PAD - 1 : PAD + FIRST], axis=AX.X, op=ALU.min)
-        nc.scalar.activation(out=e[:, 0:FIRST], in_=neg[:, PAD : PAD + FIRST], func=ACT.Exp, bias=neg_max0, scale=-1.0, accum_out=sums[:, 0:1])
-        nc.vector.tensor_reduce(out=stats[:, 0:1], in_=neg[:, PAD + FIRST : PAD + S + 1], axis=AX.X, op=ALU.min)
-        nc.scalar.activation(out=e[:, FIRST : S + 1], in_=neg[:, PAD + FIRST : PAD + S + 1], func=ACT.Exp, bias=stats[:, 0:1], scale=-1.0, accum_out=sums[:, 1:2])
-        f = e[:, S : S + 1]
-        nc.vector.tensor_scalar(out=stats[:, 1:2], in0=sums[:, 0:1], scalar1=-1.0, scalar2=None, op0=ALU.add)
-        nc.vector.tensor_scalar(out=stats[:, 2:3], in0=f, scalar1=stats[:, 1:2], scalar2=sums[:, 1:2], op0=ALU.mult, op1=ALU.add)
-        nc.vector.reciprocal(out=stats[:, 3:4], in_=stats[:, 2:3])
-        r = stats[:, 3:4]
-        for i, (lo, hi) in enumerate([(0, 256), (256, 640)]):
-            o = keep.tile([P, hi - lo], F32, name="out_v%d" % i)
-            if hi <= FIRST:
-                nc.vector.tensor_scalar(out=o[:], in0=e[:, lo:hi], scalar1=f, scalar2=r, op0=ALU.mult, op1=ALU.mult)
-            else:
-                nc.vector.tensor_scalar(out=o[:], in0=e[:, lo:hi], scalar1=r, scalar2=None, op0=ALU.mult)
-            nc.sync.dma_start(out=out[:, lo:hi], in_=o[:])
-        lo = 640
-        o = keep.tile([P, S - lo], F32, name="out_s")
-        nc.scalar.activation(out=o[:], in_=e[:, lo:S], func=ACT.Copy, scale=r)
-        nc.scalar.dma_start(out=out[:, lo:S], in_=o[:])
+        nc.vector.scalar_tensor_tensor(out=stats[:, 0:4], in0=sums[:, 0:4], scalar=-1.0, in1=e_last[:, X - 4 : X], op0=ALU.add, op1=ALU.mult, accum_out=stats[:, 4:5])
+        nc.vector.reciprocal(out=stats[:, 5:6], in_=stats[:, 4:5])
+        r = stats[:, 5:6]
+        for g in range(3):
+            o = keep.tile([P, G], F32, name="o%d" % g)
+            col = X - 3 + g
+            nc.vector.tensor_scalar(out=o[:], in0=e[g][:], scalar1=e_last[:, col : col + 1], scalar2=r, op0=ALU.mult, op1=ALU.mult)
+            nc.sync.dma_start(out=out[:, g * G : (g + 1) * G], in_=o[:])
+        o = keep.tile([P, G], F32, name="o3")
+        nc.scalar.activation(out=o[:], in_=e_last[:, X:], func=ACT.Copy, scale=r)
+        nc.scalar.dma_start(out=out[:, 3 * G :], in_=o[:])

@@ -1,6 +1,7 @@
 from contextlib import ExitStack
 
 import concourse.mybir as mybir
+from concourse.masks import make_identity
 
 K, T, S, M = 512, 2048, 1024, 128
 FLOPS = 2 * K * M * S
@@ -32,14 +33,26 @@ def tile_picked_rank_prior_p_kernel(tc, x_words, x_scales, w1, prior, offs, out)
         word_table = keep.tile([P, T], U32, name="word_table", align_bytes=64)
         w_raw = keep.tile([P, 4, M], F32, name="w_raw")
         prior_sb = keep.tile([P, S], F32, name="prior_sb")
+        prior_col = keep.tile([P, 8], F32, name="prior_col")
 
         nc.vector.memset(scale_table[:].bitcast(I32), 0)
         nc.sync.dma_start(out=w_raw[:], in_=w1.rearrange("(p j) m -> p j m", j=4))
         nc.sync.dma_start(offsets[:], offs)
-        for q in range(4):
-            nc.sync.dma_start(out=scale_table[q:P:32, :].bitcast(I32), in_=x_scales[0, q:16:4, :].bitcast(I32))
+        nc.sync.dma_start(out=prior_col[:], in_=prior[0].rearrange("(p c) -> p c", c=8))
+        nc.sync.dma_start(out=scale_table[0:P:8, :].bitcast(I32), in_=x_scales[0].bitcast(I32))
         nc.sync.dma_start(out=word_table[:].bitcast(I32), in_=x_words[0].rearrange("p n t -> p (n t)").bitcast(I32))
-        nc.sync.dma_start(out=prior_sb[:], in_=prior)
+
+        x_bytes = [keep.tile([P, 2 * G], U8, name="x_bytes%d" % h, align_bytes=64) for h in range(2)]
+        for h in range(2):
+            nc.vector.memset(x_bytes[h][:].bitcast(I32), 0)
+        ident = keep.tile([P, P], F32, name="ident")
+        nc.vector.memset(ident[:], 0.0)
+        make_identity(nc, ident[:], nomemset=True)
+        for h in range(2):
+            spread = psum.tile([P, 4, P], F32, name="spread%d" % h)
+            for c in range(4):
+                nc.tensor.transpose(spread[:, c, :], prior_col[:, 4 * h + c : 4 * h + c + 1].to_broadcast([P, P]), ident[:])
+            nc.scalar.copy(out=prior_sb[:].rearrange("q (p c) -> q p c", c=8)[:, :, 4 * h : 4 * h + 4], in_=spread[:].rearrange("q c p -> q p c"))
 
         w_bf = keep.tile([P, M, 4], BF16, name="w_bf", align_bytes=64)
         w_codes = keep.tile([P, M], U32, name="w_codes", align_bytes=64)
@@ -50,15 +63,18 @@ def tile_picked_rank_prior_p_kernel(tc, x_words, x_scales, w1, prior, offs, out)
         for m in halves:
             nc.vector.quantize_mx(out=w_codes[:, m].bitcast(FP8X4), scales=w_scales[:, m], in_=w_bf[:, m, :].rearrange("p m j -> p (m j)"))
 
-        x_bytes = keep.tile([P, S], U8, name="x_bytes", align_bytes=64)
-        nc.vector.tensor_copy(x_bytes[:], scale_table[:].indirect(offsets[:]))
+        for h in range(2):
+            picked = keep.tile([P, 2 * G], U8, name="picked%d" % h, align_bytes=64)
+            nc.vector.tensor_copy(picked[:], scale_table[:].indirect(offsets[:, h * 2 * G // 16 : (h + 1) * 2 * G // 16]))
+            for r in range(4):
+                nc.sync.dma_start(out=x_bytes[h][r:P:32, :].bitcast(I32), in_=picked[8 * r : P : 32, :].bitcast(I32))
 
         banks = []
         for c, (lo, n) in enumerate([(g * G, G) for g in range(4)]):
             codes = keep.tile([P, n], U32, name="codes%d" % c, align_bytes=64)
             nc.vector.tensor_copy(codes[:], word_table[:].indirect(offsets[:, lo // 16 : (lo + n) // 16]))
             bank = psum.tile([P, n], F32, name="bank%d" % c)
-            nc.tensor.matmul_mx(out=bank[:], lhsT=w_codes[:].bitcast(FP8X4), lhsT_scale=w_scales[:], rhs=codes[:].bitcast(FP8X4), rhs_scale=x_bytes[:, lo : lo + n], start=True, stop=True)
+            nc.tensor.matmul_mx(out=bank[:], lhsT=w_codes[:].bitcast(FP8X4), lhsT_scale=w_scales[:], rhs=codes[:].bitcast(FP8X4), rhs_scale=x_bytes[c // 2][:, (c % 2) * G : (c % 2 + 1) * G], start=True, stop=True)
             banks.append(bank)
 
         neg_y = [keep.tile([P, X + G], F32, name="neg_y%d" % g, tag="scores%d" % g) for g in range(2)]

@@ -29,7 +29,7 @@ def tile_picked_rank_prior_p_kernel(tc, x_words, x_scales, w1, prior, offs, out)
         psum = ctx.enter_context(tc.psum_pool(name="psum", bufs=1))
 
         offsets = keep.tile([P, S // 16], U16, name="offsets")
-        scale_table = keep.tile([P, T], U8, name="scale_table", align_bytes=64)
+        scale_table = keep.tile([P, T], U8, name="scale_table", tag="scale_bytes", align_bytes=64)
         word_table = keep.tile([P, T], U32, name="word_table", align_bytes=64)
         w_raw = keep.tile([P, 4, M], F32, name="w_raw")
         prior_sb = keep.tile([P, S], F32, name="prior_sb")
@@ -41,6 +41,10 @@ def tile_picked_rank_prior_p_kernel(tc, x_words, x_scales, w1, prior, offs, out)
         nc.sync.dma_start(out=prior_col[:], in_=prior[0].rearrange("(p c) -> p c", c=8))
         nc.sync.dma_start(out=scale_table[0:P:8, :].bitcast(I32), in_=x_scales[0].bitcast(I32))
         nc.sync.dma_start(out=word_table[:].bitcast(I32), in_=x_words[0].rearrange("p n t -> p (n t)").bitcast(I32))
+
+        w_bf = keep.tile([P, M, 4], BF16, name="w_bf", align_bytes=64)
+        w_codes = keep.tile([P, M], U32, name="w_codes", align_bytes=64)
+        nc.scalar.copy(out=w_bf[:].rearrange("p (c i) j -> p c j i", i=4), in_=w_raw[:].rearrange("p j (c i) -> p c j i", i=4))
 
         x_bytes = [keep.tile([P, 2 * G], U8, name="x_bytes%d" % h, align_bytes=64) for h in range(2)]
         for h in range(2):
@@ -54,35 +58,29 @@ def tile_picked_rank_prior_p_kernel(tc, x_words, x_scales, w1, prior, offs, out)
                 nc.tensor.transpose(spread[:, c, :], prior_col[:, 4 * h + c : 4 * h + c + 1].to_broadcast([P, P]), ident[:])
             nc.scalar.copy(out=prior_sb[:].rearrange("q (p c) -> q p c", c=8)[:, :, 4 * h : 4 * h + 4], in_=spread[:].rearrange("q c p -> q p c"))
 
-        w_bf = keep.tile([P, M, 4], BF16, name="w_bf", align_bytes=64)
-        w_codes = keep.tile([P, M], U32, name="w_codes", align_bytes=64)
-        w_scales = keep.tile([P, M], U8, name="w_scales", align_bytes=64)
-        halves = [slice(0, M // 2), slice(M // 2, M)]
-        for m in halves:
-            nc.vector.tensor_copy(out=w_bf[:, m, :].rearrange("p (c i) j -> p c j i", i=4), in_=w_raw[:, :, m].rearrange("p j (c i) -> p c j i", i=4))
-        for m in halves:
-            nc.vector.quantize_mx(out=w_codes[:, m].bitcast(FP8X4), scales=w_scales[:, m], in_=w_bf[:, m, :].rearrange("p m j -> p (m j)"))
-
         for h in range(2):
             picked = keep.tile([P, 2 * G], U8, name="picked%d" % h, align_bytes=64)
             nc.vector.tensor_copy(picked[:], scale_table[:].indirect(offsets[:, h * 2 * G // 16 : (h + 1) * 2 * G // 16]))
             for r in range(4):
                 nc.sync.dma_start(out=x_bytes[h][r:P:32, :].bitcast(I32), in_=picked[8 * r : P : 32, :].bitcast(I32))
 
+        w_scales = keep.tile([P, M], U8, name="w_scales", tag="scale_bytes", align_bytes=64)
+        nc.vector.quantize_mx(out=w_codes[:].bitcast(FP8X4), scales=w_scales[:], in_=w_bf[:].rearrange("p m j -> p (m j)"))
+
         banks = []
         for c, (lo, n) in enumerate([(g * G, G) for g in range(4)]):
-            codes = keep.tile([P, n], U32, name="codes%d" % c, align_bytes=64)
+            codes = keep.tile([P, n], U32, name="codes%d" % c, tag="piece%d" % c, align_bytes=64)
             nc.vector.tensor_copy(codes[:], word_table[:].indirect(offsets[:, lo // 16 : (lo + n) // 16]))
             bank = psum.tile([P, n], F32, name="bank%d" % c)
             nc.tensor.matmul_mx(out=bank[:], lhsT=w_codes[:].bitcast(FP8X4), lhsT_scale=w_scales[:], rhs=codes[:].bitcast(FP8X4), rhs_scale=x_bytes[c // 2][:, (c % 2) * G : (c % 2 + 1) * G], start=True, stop=True)
             banks.append(bank)
 
-        neg_y = [keep.tile([P, X + G], F32, name="neg_y%d" % g, tag="scores%d" % g) for g in range(2)]
+        neg_y = [keep.tile([P, X + G], F32, name="neg_y%d" % g) for g in range(2)]
         neg = [keep.tile([P, G], F32, name="neg%d" % g) for g in range(3)]
         for g in range(2):
             nc.scalar.activation(out=neg_y[g][:, X:], in_=banks[g][:], func=ACT.Copy, scale=-1.0)
             nc.gpsimd.tensor_tensor(out=neg[g][:], in0=neg_y[g][:, X:], in1=prior_sb[:, g * G : (g + 1) * G], op=ALU.subtract)
-        neg_last = keep.tile([P, X + G], F32, name="neg_last", tag="scores0")
+        neg_last = keep.tile([P, X + G], F32, name="neg_last", tag="piece2", align_bytes=64)
         e = [keep.tile([P, G], F32, name="e%d" % g) for g in range(3)]
         e_last = keep.tile([P, X + G], F32, name="e_last")
         sums = keep.tile([P, 8], F32, name="sums")

@@ -20,6 +20,7 @@ AX = mybir.AxisListType
 P = 128
 G = 256
 X = 8
+ROWS_AT = 112
 
 
 def tile_picked_rank_prior_p_kernel(tc, x_words, x_scales, w1, prior, offs, out):
@@ -35,11 +36,12 @@ def tile_picked_rank_prior_p_kernel(tc, x_words, x_scales, w1, prior, offs, out)
         prior_sb = keep.tile([P, S], F32, name="prior_sb")
         prior_col = keep.tile([P, 8], F32, name="prior_col")
 
-        nc.vector.memset(scale_table[:].bitcast(I32), 0)
-        nc.sync.dma_start(out=w_raw[:], in_=w1.rearrange("(p j) m -> p j m", j=4))
+        for lo, hi in ((0, 64), (64, 96), (96, ROWS_AT)):
+            nc.vector.memset(scale_table[lo:hi, :].bitcast(I32), 0)
+        nc.sync.dma_start(out=scale_table[ROWS_AT:P, :].bitcast(I32), in_=x_scales[0].bitcast(I32))
         nc.sync.dma_start(offsets[:], offs)
+        nc.sync.dma_start(out=w_raw[:], in_=w1.rearrange("(p j) m -> p j m", j=4))
         nc.sync.dma_start(out=prior_col[:], in_=prior[0].rearrange("(p c) -> p c", c=8))
-        nc.sync.dma_start(out=scale_table[0:P:8, :].bitcast(I32), in_=x_scales[0].bitcast(I32))
         nc.sync.dma_start(out=word_table[:].bitcast(I32), in_=x_words[0].rearrange("p n t -> p (n t)").bitcast(I32))
 
         w_bf = keep.tile([P, M, 4], BF16, name="w_bf", align_bytes=64)
@@ -62,7 +64,7 @@ def tile_picked_rank_prior_p_kernel(tc, x_words, x_scales, w1, prior, offs, out)
             picked = keep.tile([P, 2 * G], U8, name="picked%d" % h, align_bytes=64)
             nc.vector.tensor_copy(picked[:], scale_table[:].indirect(offsets[:, h * 2 * G // 16 : (h + 1) * 2 * G // 16]))
             for r in range(4):
-                nc.sync.dma_start(out=x_bytes[h][r:P:32, :].bitcast(I32), in_=picked[8 * r : P : 32, :].bitcast(I32))
+                nc.sync.dma_start(out=x_bytes[h][r:P:32, :].bitcast(I32), in_=picked[ROWS_AT + r : P : 4, :].bitcast(I32))
 
         w_scales = keep.tile([P, M], U8, name="w_scales", tag="scale_bytes", align_bytes=64)
         nc.vector.quantize_mx(out=w_codes[:].bitcast(FP8X4), scales=w_scales[:], in_=w_bf[:].rearrange("p m j -> p (m j)"))

@@ -33,15 +33,14 @@ def tile_picked_rank_prior_p_kernel(tc, x_words, x_scales, w1, prior, offs, out)
         scale_table = keep.tile([P, T], U8, name="scale_table", tag="scale_bytes", align_bytes=64)
         word_table = keep.tile([P, T], U32, name="word_table", align_bytes=64)
         w_raw = keep.tile([P, 4, M], F32, name="w_raw")
-        prior_sb = keep.tile([P, S], F32, name="prior_sb")
-        prior_col = keep.tile([P, 8], F32, name="prior_col")
+        prior_runs = keep.tile([P, 8], F32, name="prior_runs")
 
         for lo, hi in ((0, 64), (64, 96), (96, ROWS_AT)):
             nc.vector.memset(scale_table[lo:hi, :].bitcast(I32), 0)
         nc.sync.dma_start(out=scale_table[ROWS_AT:P, :].bitcast(I32), in_=x_scales[0].bitcast(I32))
         nc.sync.dma_start(offsets[:], offs)
         nc.sync.dma_start(out=w_raw[:], in_=w1.rearrange("(p j) m -> p j m", j=4))
-        nc.sync.dma_start(out=prior_col[:], in_=prior[0].rearrange("(p c) -> p c", c=8))
+        nc.sync.dma_start(out=prior_runs[:], in_=prior[0].rearrange("(p c) -> p c", c=8))
         nc.sync.dma_start(out=word_table[:].bitcast(I32), in_=x_words[0].rearrange("p n t -> p (n t)").bitcast(I32))
 
         w_bf = keep.tile([P, M, 4], BF16, name="w_bf", align_bytes=64)
@@ -54,11 +53,18 @@ def tile_picked_rank_prior_p_kernel(tc, x_words, x_scales, w1, prior, offs, out)
         ident = keep.tile([P, P], F32, name="ident")
         nc.vector.memset(ident[:], 0.0)
         make_identity(nc, ident[:], nomemset=True)
+
+        prior_rows = keep.tile([P, S], F32, name="prior_rows")
         for h in range(2):
-            spread = psum.tile([P, 4, P], F32, name="spread%d" % h)
+            spread = psum.tile([P, 4, P], F32, name="spread%d" % h, tag=("back", "direct0")[h])
             for c in range(4):
-                nc.tensor.transpose(spread[:, c, :], prior_col[:, 4 * h + c : 4 * h + c + 1].to_broadcast([P, P]), ident[:])
-            nc.scalar.copy(out=prior_sb[:].rearrange("q (p c) -> q p c", c=8)[:, :, 4 * h : 4 * h + 4], in_=spread[:].rearrange("q c p -> q p c"))
+                nc.tensor.transpose(spread[:, c, :], prior_runs[:, 4 * h + c : 4 * h + c + 1].to_broadcast([P, P]), ident[:])
+            nc.scalar.copy(out=prior_rows[:].rearrange("q (p c) -> q p c", c=8)[:, :, 4 * h : 4 * h + 4], in_=spread[:].rearrange("q c p -> q p c"))
+        prior_turned = psum.tile([P, 2, P], F32, name="prior_turned", tag="turned")
+        for b in range(2):
+            nc.tensor.transpose(prior_turned[:, b, :], prior_rows[:, G + b * P : G + (b + 1) * P], ident[:])
+        neg_prior = keep.tile([P, 2], F32, name="neg_prior")
+        nc.scalar.activation(out=neg_prior[:], in_=prior_turned[:, :, 0], func=ACT.Copy, scale=-1.0)
 
         for h in range(2):
             picked = keep.tile([P, 2 * G], U8, name="picked%d" % h, align_bytes=64)
@@ -69,32 +75,46 @@ def tile_picked_rank_prior_p_kernel(tc, x_words, x_scales, w1, prior, offs, out)
         w_scales = keep.tile([P, M], U8, name="w_scales", tag="scale_bytes", align_bytes=64)
         nc.vector.quantize_mx(out=w_codes[:].bitcast(FP8X4), scales=w_scales[:], in_=w_bf[:].rearrange("p m j -> p (m j)"))
 
-        banks = []
-        for c, (lo, n) in enumerate([(g * G, G) for g in range(4)]):
-            codes = keep.tile([P, n], U32, name="codes%d" % c, tag="piece%d" % c, align_bytes=64)
-            nc.vector.tensor_copy(codes[:], word_table[:].indirect(offsets[:, lo // 16 : (lo + n) // 16]))
-            bank = psum.tile([P, n], F32, name="bank%d" % c)
-            nc.tensor.matmul_mx(out=bank[:], lhsT=w_codes[:].bitcast(FP8X4), lhsT_scale=w_scales[:], rhs=codes[:].bitcast(FP8X4), rhs_scale=x_bytes[c // 2][:, (c % 2) * G : (c % 2 + 1) * G], start=True, stop=True)
-            banks.append(bank)
+        codes = []
+        for c in range(4):
+            piece = keep.tile([P, G], U32, name="codes%d" % c, tag="piece%d" % c, align_bytes=64)
+            nc.vector.tensor_copy(piece[:], word_table[:].indirect(offsets[:, c * G // 16 : (c + 1) * G // 16]))
+            codes.append(piece)
 
-        neg_y = [keep.tile([P, X + G], F32, name="neg_y%d" % g) for g in range(2)]
-        neg = [keep.tile([P, G], F32, name="neg%d" % g) for g in range(3)]
-        for g in range(2):
-            nc.scalar.activation(out=neg_y[g][:, X:], in_=banks[g][:], func=ACT.Copy, scale=-1.0)
-            nc.gpsimd.tensor_tensor(out=neg[g][:], in0=neg_y[g][:, X:], in1=prior_sb[:, g * G : (g + 1) * G], op=ALU.subtract)
+        blocks = keep.tile([P, G], F32, name="blocks")
+        turned = psum.tile([P, G], F32, name="turned", tag="turned")
+        for b in range(2):
+            cols = slice(b * P, (b + 1) * P)
+            nc.tensor.matmul_mx(out=turned[:, cols], lhsT=codes[1][:, cols].bitcast(FP8X4), lhsT_scale=x_bytes[0][:, G + b * P : G + (b + 1) * P], rhs=w_codes[:].bitcast(FP8X4), rhs_scale=w_scales[:], start=True, stop=True)
+        for b in range(2):
+            cols = slice(b * P, (b + 1) * P)
+            nc.scalar.activation(out=blocks[:, cols], in_=turned[:, cols], func=ACT.Identity, bias=neg_prior[:, b : b + 1], scale=-1.0)
+        direct = {}
+        for g in (0, 2, 3):
+            bank = psum.tile([P, G], F32, name="direct%d" % g, tag="direct%d" % g)
+            nc.tensor.matmul_mx(out=bank[:], lhsT=w_codes[:].bitcast(FP8X4), lhsT_scale=w_scales[:], rhs=codes[g][:].bitcast(FP8X4), rhs_scale=x_bytes[g // 2][:, (g % 2) * G : (g % 2 + 1) * G], start=True, stop=True)
+            direct[g] = bank
+        back = psum.tile([P, G], F32, name="back", tag="back")
+        for b in range(2):
+            nc.tensor.transpose(back[:, b * P : (b + 1) * P], blocks[:, b * P : (b + 1) * P], ident[:])
+
+        neg = [keep.tile([P, G], F32, name="neg0"), back, keep.tile([P, G], F32, name="neg2")]
         neg_last = keep.tile([P, X + G], F32, name="neg_last", tag="piece2", align_bytes=64)
         e = [keep.tile([P, G], F32, name="e%d" % g) for g in range(3)]
         e_last = keep.tile([P, X + G], F32, name="e_last")
         sums = keep.tile([P, 8], F32, name="sums")
 
         def add_prior(g, dst):
-            nc.vector.scalar_tensor_tensor(out=dst, in0=banks[g][:], scalar=-1.0, in1=prior_sb[:, g * G : (g + 1) * G], op0=ALU.mult, op1=ALU.subtract)
+            nc.vector.scalar_tensor_tensor(out=dst, in0=direct[g][:], scalar=-1.0, in1=prior_rows[:, g * G : (g + 1) * G], op0=ALU.mult, op1=ALU.subtract)
 
         def own_softmax(g):
             col = X - 3 + g
             nc.vector.tensor_reduce(out=neg_last[:, col : col + 1], in_=neg[g][:], axis=AX.X, op=ALU.min)
             nc.scalar.activation(out=e[g][:], in_=neg[g][:], func=ACT.Exp, bias=neg_last[:, col : col + 1], scale=-1.0, accum_out=sums[:, 1 + g : 2 + g])
 
+        neg_y = keep.tile([P, G], F32, name="neg_y")
+        nc.scalar.activation(out=neg_y[:], in_=direct[0][:], func=ACT.Copy, scale=-1.0)
+        nc.gpsimd.tensor_tensor(out=neg[0][:], in0=neg_y[:], in1=prior_rows[:, :G], op=ALU.subtract)
         add_prior(2, neg[2][:])
         own_softmax(0)
         own_softmax(2)

@@ -35,8 +35,12 @@ def tile_picked_rank_prior_p_kernel(tc, x_words, x_scales, w1, prior, offs, out)
         w_raw = keep.tile([P, 4, M], F32, name="w_raw")
         prior_runs = keep.tile([P, 8], F32, name="prior_runs")
 
-        for lo, hi in ((0, 64), (64, 96), (96, ROWS_AT)):
+        for lo, hi in ((0, 64), (64, 96)):
             nc.vector.memset(scale_table[lo:hi, :].bitcast(I32), 0)
+        ident = keep.tile([P, P], F32, name="ident")
+        nc.vector.memset(ident[:], 0.0)
+        make_identity(nc, ident[:], nomemset=True)
+        nc.vector.memset(scale_table[96:ROWS_AT, :].bitcast(I32), 0)
         nc.sync.dma_start(out=scale_table[ROWS_AT:P, :].bitcast(I32), in_=x_scales[0].bitcast(I32))
         nc.sync.dma_start(offsets[:], offs)
         nc.sync.dma_start(out=w_raw[:], in_=w1.rearrange("(p j) m -> p j m", j=4))
@@ -50,9 +54,6 @@ def tile_picked_rank_prior_p_kernel(tc, x_words, x_scales, w1, prior, offs, out)
         x_bytes = [keep.tile([P, 2 * G], U8, name="x_bytes%d" % h, align_bytes=64) for h in range(2)]
         for h in range(2):
             nc.vector.memset(x_bytes[h][:].bitcast(I32), 0)
-        ident = keep.tile([P, P], F32, name="ident")
-        nc.vector.memset(ident[:], 0.0)
-        make_identity(nc, ident[:], nomemset=True)
 
         prior_rows = keep.tile([P, S], F32, name="prior_rows")
         for h in range(2):

@@ -21,6 +21,7 @@ P = 128
 G = 256
 X = 8
 ROWS_AT = 112
+BIG = 2.0**126
 
 
 def tile_picked_rank_prior_p_kernel(tc, x_words, x_scales, w1, prior, offs, out):
@@ -47,6 +48,9 @@ def tile_picked_rank_prior_p_kernel(tc, x_words, x_scales, w1, prior, offs, out)
         nc.sync.dma_start(out=prior_runs[:], in_=prior[0].rearrange("(p c) -> p c", c=8))
         nc.sync.dma_start(out=word_table[:].bitcast(I32), in_=x_words[0].rearrange("p n t -> p (n t)").bitcast(I32))
 
+        prior_floor = keep.tile([P, 8], F32, name="prior_floor")
+        nc.gpsimd.tensor_scalar(out=prior_floor[:], in0=prior_runs[:], scalar1=BIG, scalar2=-BIG, op0=ALU.min, op1=ALU.max)
+
         w_bf = keep.tile([P, M, 4], BF16, name="w_bf", align_bytes=64)
         w_codes = keep.tile([P, M], U32, name="w_codes", align_bytes=64)
         nc.scalar.copy(out=w_bf[:].rearrange("p (c i) j -> p c j i", i=4), in_=w_raw[:].rearrange("p j (c i) -> p c j i", i=4))
@@ -59,7 +63,7 @@ def tile_picked_rank_prior_p_kernel(tc, x_words, x_scales, w1, prior, offs, out)
         for h in range(2):
             spread = psum.tile([P, 4, P], F32, name="spread%d" % h, tag=("back", "direct0")[h])
             for c in range(4):
-                nc.tensor.transpose(spread[:, c, :], prior_runs[:, 4 * h + c : 4 * h + c + 1].to_broadcast([P, P]), ident[:])
+                nc.tensor.transpose(spread[:, c, :], prior_floor[:, 4 * h + c : 4 * h + c + 1].to_broadcast([P, P]), ident[:])
             nc.scalar.copy(out=prior_rows[:].rearrange("q (p c) -> q p c", c=8)[:, :, 4 * h : 4 * h + 4], in_=spread[:].rearrange("q c p -> q p c"))
         prior_turned = psum.tile([P, 2, P], F32, name="prior_turned", tag="turned")
         for b in range(2):

@@ -139,4 +139,4 @@ def tile_picked_rank_prior_p_kernel(tc, x_words, x_scales, w1, prior, offs, out)
             nc.sync.dma_start(out=out[:, g * G : (g + 1) * G], in_=o[:])
         o = keep.tile([P, G], F32, name="o3")
         nc.scalar.activation(out=o[:], in_=e_last[:, X:], func=ACT.Copy, scale=r)
-        nc.scalar.dma_start(out=out[:, 3 * G :], in_=o[:])
+        nc.sync.dma_start(out=out[:, 3 * G :], in_=o[:])

@@ -132,11 +132,10 @@ def tile_picked_rank_prior_p_kernel(tc, x_words, x_scales, w1, prior, offs, out)
         nc.vector.scalar_tensor_tensor(out=stats[:, 0:4], in0=sums[:, 0:4], scalar=-1.0, in1=e_last[:, X - 4 : X], op0=ALU.add, op1=ALU.mult, accum_out=stats[:, 4:5])
         nc.vector.reciprocal(out=stats[:, 5:6], in_=stats[:, 4:5])
         r = stats[:, 5:6]
+        o = keep.tile([P, S], F32, name="o")
         for g in range(3):
-            o = keep.tile([P, G], F32, name="o%d" % g)
             col = X - 3 + g
-            nc.vector.tensor_scalar(out=o[:], in0=e[g][:], scalar1=e_last[:, col : col + 1], scalar2=r, op0=ALU.mult, op1=ALU.mult)
-            nc.sync.dma_start(out=out[:, g * G : (g + 1) * G], in_=o[:])
-        o = keep.tile([P, G], F32, name="o3")
-        nc.scalar.activation(out=o[:], in_=e_last[:, X:], func=ACT.Copy, scale=r)
-        nc.sync.dma_start(out=out[:, 3 * G :], in_=o[:])
+            nc.vector.tensor_scalar(out=o[:, g * G : (g + 1) * G], in0=e[g][:], scalar1=e_last[:, col : col + 1], scalar2=r, op0=ALU.mult, op1=ALU.mult)
+        nc.scalar.activation(out=o[:, 3 * G :], in_=e_last[:, X:], func=ACT.Copy, scale=r)
+        nc.sync.dma_start(out=out[:, :G], in_=o[:, :G])
+        nc.sync.dma_start(out=out[:, G:], in_=o[:, G:])

@@ -22,6 +22,7 @@ G = 256
 X = 8
 ROWS_AT = 112
 BIG = 2.0**126
+CUT = 384
 
 
 def tile_picked_rank_prior_p_kernel(tc, x_words, x_scales, w1, prior, offs, out):
@@ -55,7 +56,12 @@ def tile_picked_rank_prior_p_kernel(tc, x_words, x_scales, w1, prior, offs, out)
         w_codes = keep.tile([P, M], U32, name="w_codes", align_bytes=64)
         nc.scalar.copy(out=w_bf[:].rearrange("p (c i) j -> p c j i", i=4), in_=w_raw[:].rearrange("p j (c i) -> p c j i", i=4))
 
-        x_bytes = [keep.tile([P, 2 * G], U8, name="x_bytes%d" % h, align_bytes=64) for h in range(2)]
+        spans = ((0, CUT), (CUT, S))
+        x_bytes = [keep.tile([P, hi - lo], U8, name="x_bytes%d" % lo, align_bytes=64) for lo, hi in spans]
+
+        def byte_cols(lo, hi):
+            return x_bytes[0][:, lo:hi] if hi <= CUT else x_bytes[1][:, lo - CUT : hi - CUT]
+
         for h in range(2):
             nc.vector.memset(x_bytes[h][:].bitcast(I32), 0)
 
@@ -71,9 +77,9 @@ def tile_picked_rank_prior_p_kernel(tc, x_words, x_scales, w1, prior, offs, out)
         neg_prior = keep.tile([P, 2], F32, name="neg_prior")
         nc.scalar.activation(out=neg_prior[:], in_=prior_turned[:, :, 0], func=ACT.Copy, scale=-1.0)
 
-        for h in range(2):
-            picked = keep.tile([P, 2 * G], U8, name="picked%d" % h, align_bytes=64)
-            nc.vector.tensor_copy(picked[:], scale_table[:].indirect(offsets[:, h * 2 * G // 16 : (h + 1) * 2 * G // 16]))
+        for h, (lo, hi) in enumerate(spans):
+            picked = keep.tile([P, hi - lo], U8, name="picked%d" % h, align_bytes=64)
+            nc.vector.tensor_copy(picked[:], scale_table[:].indirect(offsets[:, lo // 16 : hi // 16]))
             for r in range(4):
                 nc.sync.dma_start(out=x_bytes[h][r:P:32, :].bitcast(I32), in_=picked[ROWS_AT + r : P : 4, :].bitcast(I32))
 
@@ -81,24 +87,29 @@ def tile_picked_rank_prior_p_kernel(tc, x_words, x_scales, w1, prior, offs, out)
         nc.vector.quantize_mx(out=w_codes[:].bitcast(FP8X4), scales=w_scales[:], in_=w_bf[:].rearrange("p m j -> p (m j)"))
 
         codes = []
-        for c in range(4):
-            piece = keep.tile([P, G], U32, name="codes%d" % c, tag="piece%d" % c, align_bytes=64)
-            nc.vector.tensor_copy(piece[:], word_table[:].indirect(offsets[:, c * G // 16 : (c + 1) * G // 16]))
+        for c, (lo, hi) in enumerate(((0, G), (G, 2 * G), (2 * G, 3 * G), (3 * G, 3 * G + P), (3 * G + P, S))):
+            piece = keep.tile([P, hi - lo], U32, name="codes%d" % c, tag="piece%d" % c, align_bytes=64)
+            nc.vector.tensor_copy(piece[:], word_table[:].indirect(offsets[:, lo // 16 : hi // 16]))
             codes.append(piece)
 
         blocks = keep.tile([P, G], F32, name="blocks")
         turned = psum.tile([P, G], F32, name="turned", tag="turned")
         for b in range(2):
             cols = slice(b * P, (b + 1) * P)
-            nc.tensor.matmul_mx(out=turned[:, cols], lhsT=codes[1][:, cols].bitcast(FP8X4), lhsT_scale=x_bytes[0][:, G + b * P : G + (b + 1) * P], rhs=w_codes[:].bitcast(FP8X4), rhs_scale=w_scales[:], start=True, stop=True)
+            nc.tensor.matmul_mx(out=turned[:, cols], lhsT=codes[1][:, cols].bitcast(FP8X4), lhsT_scale=byte_cols(G + b * P, G + (b + 1) * P), rhs=w_codes[:].bitcast(FP8X4), rhs_scale=w_scales[:], start=True, stop=True)
         for b in range(2):
             cols = slice(b * P, (b + 1) * P)
             nc.scalar.activation(out=blocks[:, cols], in_=turned[:, cols], func=ACT.Identity, bias=neg_prior[:, b : b + 1], scale=-1.0)
         direct = {}
-        for g in (0, 2, 3):
+        for g in (0, 2):
             bank = psum.tile([P, G], F32, name="direct%d" % g, tag="direct%d" % g)
-            nc.tensor.matmul_mx(out=bank[:], lhsT=w_codes[:].bitcast(FP8X4), lhsT_scale=w_scales[:], rhs=codes[g][:].bitcast(FP8X4), rhs_scale=x_bytes[g // 2][:, (g % 2) * G : (g % 2 + 1) * G], start=True, stop=True)
+            nc.tensor.matmul_mx(out=bank[:], lhsT=w_codes[:].bitcast(FP8X4), lhsT_scale=w_scales[:], rhs=codes[g][:].bitcast(FP8X4), rhs_scale=byte_cols(g * G, (g + 1) * G), start=True, stop=True)
             direct[g] = bank
+        halves = []
+        for b in range(2):
+            bank = psum.tile([P, P], F32, name="half%d" % b)
+            nc.tensor.matmul_mx(out=bank[:], lhsT=w_codes[:].bitcast(FP8X4), lhsT_scale=w_scales[:], rhs=codes[3 + b][:].bitcast(FP8X4), rhs_scale=byte_cols(3 * G + b * P, 3 * G + (b + 1) * P), start=True, stop=True)
+            halves.append(bank)
         back = psum.tile([P, G], F32, name="back", tag="back")
         for b in range(2):
             nc.tensor.transpose(back[:, b * P : (b + 1) * P], blocks[:, b * P : (b + 1) * P], ident[:])
@@ -120,10 +131,13 @@ def tile_picked_rank_prior_p_kernel(tc, x_words, x_scales, w1, prior, offs, out)
         neg_y = keep.tile([P, G], F32, name="neg_y")
         nc.scalar.activation(out=neg_y[:], in_=direct[0][:], func=ACT.Copy, scale=-1.0)
         nc.gpsimd.tensor_tensor(out=neg[0][:], in0=neg_y[:], in1=prior_rows[:, :G], op=ALU.subtract)
+        neg_half = keep.tile([P, P], F32, name="neg_half")
+        nc.scalar.activation(out=neg_half[:], in_=halves[0][:], func=ACT.Copy, scale=-1.0)
+        nc.gpsimd.tensor_tensor(out=neg_last[:, X : X + P], in0=neg_half[:], in1=prior_rows[:, 3 * G : 3 * G + P], op=ALU.subtract)
         add_prior(2, neg[2][:])
         own_softmax(0)
         own_softmax(2)
-        add_prior(3, neg_last[:, X:])
+        nc.vector.scalar_tensor_tensor(out=neg_last[:, X + P :], in0=halves[1][:], scalar=-1.0, in1=prior_rows[:, 3 * G + P :], op0=ALU.mult, op1=ALU.subtract)
         own_softmax(1)
         nc.vector.tensor_reduce(out=neg_last[:, X - 4 : X - 3], in_=neg_last[:, X - 3 :], axis=AX.X, op=ALU.min)
         nc.scalar.activation(out=e_last[:, X - 4 :], in_=neg_last[:, X - 4 :], func=ACT.Exp, bias=neg_last[:, X - 4 : X - 3], scale=-1.0, accum_out=sums[:, 0:1])

@@ -139,17 +139,21 @@ def tile_picked_rank_prior_p_kernel(tc, x_words, x_scales, w1, prior, offs, out)
         own_softmax(2)
         nc.vector.scalar_tensor_tensor(out=neg_last[:, X + P :], in0=halves[1][:], scalar=-1.0, in1=prior_rows[:, 3 * G + P :], op0=ALU.mult, op1=ALU.subtract)
         own_softmax(1)
-        nc.vector.tensor_reduce(out=neg_last[:, X - 4 : X - 3], in_=neg_last[:, X - 3 :], axis=AX.X, op=ALU.min)
-        nc.scalar.activation(out=e_last[:, X - 4 :], in_=neg_last[:, X - 4 :], func=ACT.Exp, bias=neg_last[:, X - 4 : X - 3], scale=-1.0, accum_out=sums[:, 0:1])
+        nc.vector.tensor_reduce(out=neg_last[:, X - 4 : X - 3], in_=neg_last[:, X:], axis=AX.X, op=ALU.min)
+        nc.scalar.activation(out=e_last[:, X:], in_=neg_last[:, X:], func=ACT.Exp, bias=neg_last[:, X - 4 : X - 3], scale=-1.0, accum_out=sums[:, 0:1])
+        nc.vector.tensor_reduce(out=neg_last[:, X - 5 : X - 4], in_=neg_last[:, X - 4 : X], axis=AX.X, op=ALU.min)
+        nc.scalar.activation(out=e_last[:, X - 4 : X], in_=neg_last[:, X - 4 : X], func=ACT.Exp, bias=neg_last[:, X - 5 : X - 4], scale=-1.0)
+        e_moved = keep.tile([P, G], F32, name="e_moved")
+        nc.scalar.activation(out=e_moved[:], in_=e_last[:, X:], func=ACT.Copy, scale=e_last[:, X - 4 : X - 3])
 
         stats = keep.tile([P, 8], F32, name="stats")
-        nc.vector.scalar_tensor_tensor(out=stats[:, 0:4], in0=sums[:, 0:4], scalar=-1.0, in1=e_last[:, X - 4 : X], op0=ALU.add, op1=ALU.mult, accum_out=stats[:, 4:5])
+        nc.vector.scalar_tensor_tensor(out=stats[:, 0:4], in0=sums[:, 0:4], scalar=1.0, in1=e_last[:, X - 4 : X], op0=ALU.mult, op1=ALU.mult, accum_out=stats[:, 4:5])
         nc.vector.reciprocal(out=stats[:, 5:6], in_=stats[:, 4:5])
         r = stats[:, 5:6]
         o = keep.tile([P, S], F32, name="o")
         for g in range(3):
             col = X - 3 + g
             nc.vector.tensor_scalar(out=o[:, g * G : (g + 1) * G], in0=e[g][:], scalar1=e_last[:, col : col + 1], scalar2=r, op0=ALU.mult, op1=ALU.mult)
-        nc.scalar.activation(out=o[:, 3 * G :], in_=e_last[:, X:], func=ACT.Copy, scale=r)
+        nc.scalar.activation(out=o[:, 3 * G :], in_=e_moved[:], func=ACT.Copy, scale=r)
         nc.sync.dma_start(out=out[:, :G], in_=o[:, :G])
         nc.sync.dma_start(out=out[:, G:], in_=o[:, G:])

from contextlib import ExitStack

import concourse.mybir as mybir
from concourse.masks import make_identity

K, T, S, M = 512, 2048, 1024, 128
FLOPS = 2 * K * M * S

F32 = mybir.dt.float32
BF16 = mybir.dt.bfloat16
I32 = mybir.dt.int32
U32 = mybir.dt.uint32
U16 = mybir.dt.uint16
U8 = mybir.dt.uint8
FP8X4 = mybir.dt.float8_e4m3fn_x4
ALU = mybir.AluOpType
ACT = mybir.ActivationFunctionType
AX = mybir.AxisListType

P = 128
G = 256
X = 8
ROWS_AT = 112
BIG = 2.0**126
CUT = 384


def tile_picked_rank_prior_p_kernel(tc, x_words, x_scales, w1, prior, offs, out):
    nc = tc.nc
    with ExitStack() as ctx:
        keep = ctx.enter_context(tc.tile_pool(name="keep", bufs=1))
        psum = ctx.enter_context(tc.psum_pool(name="psum", bufs=1))

        offsets = keep.tile([P, S // 16], U16, name="offsets")
        scale_table = keep.tile([P, T], U8, name="scale_table", tag="scale_bytes", align_bytes=64)
        word_table = keep.tile([P, T], U32, name="word_table", align_bytes=64)
        w_raw = keep.tile([P, 4, M], F32, name="w_raw")
        prior_runs = keep.tile([P, 8], F32, name="prior_runs")

        for lo, hi in ((0, 64), (64, 96)):
            nc.vector.memset(scale_table[lo:hi, :].bitcast(I32), 0)
        ident = keep.tile([P, P], F32, name="ident")
        nc.vector.memset(ident[:], 0.0)
        make_identity(nc, ident[:], nomemset=True)
        nc.vector.memset(scale_table[96:ROWS_AT, :].bitcast(I32), 0)
        nc.sync.dma_start(out=scale_table[ROWS_AT:P, :].bitcast(I32), in_=x_scales[0].bitcast(I32))
        nc.sync.dma_start(offsets[:], offs)
        nc.sync.dma_start(out=w_raw[:], in_=w1.rearrange("(p j) m -> p j m", j=4))
        nc.sync.dma_start(out=prior_runs[:], in_=prior[0].rearrange("(p c) -> p c", c=8))
        nc.sync.dma_start(out=word_table[:].bitcast(I32), in_=x_words[0].rearrange("p n t -> p (n t)").bitcast(I32))

        prior_floor = keep.tile([P, 8], F32, name="prior_floor")
        nc.gpsimd.tensor_scalar(out=prior_floor[:], in0=prior_runs[:], scalar1=BIG, scalar2=-BIG, op0=ALU.min, op1=ALU.max)

        w_bf = keep.tile([P, M, 4], BF16, name="w_bf", align_bytes=64)
        w_codes = keep.tile([P, M], U32, name="w_codes", align_bytes=64)
        nc.scalar.copy(out=w_bf[:].rearrange("p (c i) j -> p c j i", i=4), in_=w_raw[:].rearrange("p j (c i) -> p c j i", i=4))

        spans = ((0, CUT), (CUT, S))
        x_bytes = [keep.tile([P, hi - lo], U8, name="x_bytes%d" % lo, align_bytes=64) for lo, hi in spans]

        def byte_cols(lo, hi):
            return x_bytes[0][:, lo:hi] if hi <= CUT else x_bytes[1][:, lo - CUT : hi - CUT]

        for h in range(2):
            nc.vector.memset(x_bytes[h][:].bitcast(I32), 0)

        prior_rows = keep.tile([P, S], F32, name="prior_rows")
        for h in range(2):
            spread = psum.tile([P, 4, P], F32, name="spread%d" % h, tag=("back", "direct0")[h])
            for c in range(4):
                nc.tensor.transpose(spread[:, c, :], prior_floor[:, 4 * h + c : 4 * h + c + 1].to_broadcast([P, P]), ident[:])
            nc.scalar.copy(out=prior_rows[:].rearrange("q (p c) -> q p c", c=8)[:, :, 4 * h : 4 * h + 4], in_=spread[:].rearrange("q c p -> q p c"))
        prior_turned = psum.tile([P, 2, P], F32, name="prior_turned", tag="turned")
        for b in range(2):
            nc.tensor.transpose(prior_turned[:, b, :], prior_rows[:, G + b * P : G + (b + 1) * P], ident[:])
        neg_prior = keep.tile([P, 2], F32, name="neg_prior")
        nc.scalar.activation(out=neg_prior[:], in_=prior_turned[:, :, 0], func=ACT.Copy, scale=-1.0)

        for h, (lo, hi) in enumerate(spans):
            picked = keep.tile([P, hi - lo], U8, name="picked%d" % h, align_bytes=64)
            nc.vector.tensor_copy(picked[:], scale_table[:].indirect(offsets[:, lo // 16 : hi // 16]))
            for r in range(4):
                nc.sync.dma_start(out=x_bytes[h][r:P:32, :].bitcast(I32), in_=picked[ROWS_AT + r : P : 4, :].bitcast(I32))

        w_scales = keep.tile([P, M], U8, name="w_scales", tag="scale_bytes", align_bytes=64)
        nc.vector.quantize_mx(out=w_codes[:].bitcast(FP8X4), scales=w_scales[:], in_=w_bf[:].rearrange("p m j -> p (m j)"))

        codes = []
        for c, (lo, hi) in enumerate(((0, G), (G, 2 * G), (2 * G, 3 * G), (3 * G, 3 * G + P), (3 * G + P, S))):
            piece = keep.tile([P, hi - lo], U32, name="codes%d" % c, tag="piece%d" % c, align_bytes=64)
            nc.vector.tensor_copy(piece[:], word_table[:].indirect(offsets[:, lo // 16 : hi // 16]))
            codes.append(piece)

        blocks = keep.tile([P, G], F32, name="blocks")
        turned = psum.tile([P, G], F32, name="turned", tag="turned")
        for b in range(2):
            cols = slice(b * P, (b + 1) * P)
            nc.tensor.matmul_mx(out=turned[:, cols], lhsT=codes[1][:, cols].bitcast(FP8X4), lhsT_scale=byte_cols(G + b * P, G + (b + 1) * P), rhs=w_codes[:].bitcast(FP8X4), rhs_scale=w_scales[:], start=True, stop=True)
        for b in range(2):
            cols = slice(b * P, (b + 1) * P)
            nc.scalar.activation(out=blocks[:, cols], in_=turned[:, cols], func=ACT.Identity, bias=neg_prior[:, b : b + 1], scale=-1.0)
        direct = {}
        for g in (0, 2):
            bank = psum.tile([P, G], F32, name="direct%d" % g, tag="direct%d" % g)
            nc.tensor.matmul_mx(out=bank[:], lhsT=w_codes[:].bitcast(FP8X4), lhsT_scale=w_scales[:], rhs=codes[g][:].bitcast(FP8X4), rhs_scale=byte_cols(g * G, (g + 1) * G), start=True, stop=True)
            direct[g] = bank
        halves = []
        for b in range(2):
            bank = psum.tile([P, P], F32, name="half%d" % b)
            nc.tensor.matmul_mx(out=bank[:], lhsT=w_codes[:].bitcast(FP8X4), lhsT_scale=w_scales[:], rhs=codes[3 + b][:].bitcast(FP8X4), rhs_scale=byte_cols(3 * G + b * P, 3 * G + (b + 1) * P), start=True, stop=True)
            halves.append(bank)
        back = psum.tile([P, G], F32, name="back", tag="back")
        for b in range(2):
            nc.tensor.transpose(back[:, b * P : (b + 1) * P], blocks[:, b * P : (b + 1) * P], ident[:])

        neg = [keep.tile([P, G], F32, name="neg0"), back, keep.tile([P, G], F32, name="neg2")]
        neg_last = keep.tile([P, X + G], F32, name="neg_last", tag="piece2", align_bytes=64)
        e = [keep.tile([P, G], F32, name="e%d" % g) for g in range(3)]
        e_last = keep.tile([P, X + G], F32, name="e_last")
        sums = keep.tile([P, 8], F32, name="sums")

        def add_prior(g, dst):
            nc.vector.scalar_tensor_tensor(out=dst, in0=direct[g][:], scalar=-1.0, in1=prior_rows[:, g * G : (g + 1) * G], op0=ALU.mult, op1=ALU.subtract)

        def own_softmax(g):
            col = X - 3 + g
            nc.vector.tensor_reduce(out=neg_last[:, col : col + 1], in_=neg[g][:], axis=AX.X, op=ALU.min)
            nc.scalar.activation(out=e[g][:], in_=neg[g][:], func=ACT.Exp, bias=neg_last[:, col : col + 1], scale=-1.0, accum_out=sums[:, 1 + g : 2 + g])

        neg_y = keep.tile([P, G], F32, name="neg_y")
        nc.scalar.activation(out=neg_y[:], in_=direct[0][:], func=ACT.Copy, scale=-1.0)
        nc.gpsimd.tensor_tensor(out=neg[0][:], in0=neg_y[:], in1=prior_rows[:, :G], op=ALU.subtract)
        neg_half = keep.tile([P, P], F32, name="neg_half")
        nc.scalar.activation(out=neg_half[:], in_=halves[0][:], func=ACT.Copy, scale=-1.0)
        nc.gpsimd.tensor_tensor(out=neg_last[:, X : X + P], in0=neg_half[:], in1=prior_rows[:, 3 * G : 3 * G + P], op=ALU.subtract)
        add_prior(2, neg[2][:])
        own_softmax(0)
        own_softmax(2)
        nc.vector.scalar_tensor_tensor(out=neg_last[:, X + P :], in0=halves[1][:], scalar=-1.0, in1=prior_rows[:, 3 * G + P :], op0=ALU.mult, op1=ALU.subtract)
        own_softmax(1)
        nc.vector.tensor_reduce(out=neg_last[:, X - 4 : X - 3], in_=neg_last[:, X:], axis=AX.X, op=ALU.min)
        nc.scalar.activation(out=e_last[:, X:], in_=neg_last[:, X:], func=ACT.Exp, bias=neg_last[:, X - 4 : X - 3], scale=-1.0, accum_out=sums[:, 0:1])
        nc.vector.tensor_reduce(out=neg_last[:, X - 5 : X - 4], in_=neg_last[:, X - 4 : X], axis=AX.X, op=ALU.min)
        nc.scalar.activation(out=e_last[:, X - 4 : X], in_=neg_last[:, X - 4 : X], func=ACT.Exp, bias=neg_last[:, X - 5 : X - 4], scale=-1.0)
        e_moved = keep.tile([P, G], F32, name="e_moved")
        nc.scalar.activation(out=e_moved[:], in_=e_last[:, X:], func=ACT.Copy, scale=e_last[:, X - 4 : X - 3])

        stats = keep.tile([P, 8], F32, name="stats")
        nc.vector.scalar_tensor_tensor(out=stats[:, 0:4], in0=sums[:, 0:4], scalar=1.0, in1=e_last[:, X - 4 : X], op0=ALU.mult, op1=ALU.mult, accum_out=stats[:, 4:5])
        nc.vector.reciprocal(out=stats[:, 5:6], in_=stats[:, 4:5])
        r = stats[:, 5:6]
        o = keep.tile([P, S], F32, name="o")
        for g in range(3):
            col = X - 3 + g
            nc.vector.tensor_scalar(out=o[:, g * G : (g + 1) * G], in0=e[g][:], scalar1=e_last[:, col : col + 1], scalar2=r, op0=ALU.mult, op1=ALU.mult)
        nc.scalar.activation(out=o[:, 3 * G :], in_=e_moved[:], func=ACT.Copy, scale=r)
        nc.sync.dma_start(out=out[:, :G], in_=o[:, :G])
        nc.sync.dma_start(out=out[:, G:], in_=o[:, G:])
